import numpy as np
import ml_dtypes


def mxq(x, axis, fmt="e4m3"):
    dtype, down = {"e4m3": (ml_dtypes.float8_e4m3fn, 7), "e5m2": (ml_dtypes.float8_e5m2, 14)}[fmt]
    v = np.moveaxis(np.asarray(x, np.float32).astype(ml_dtypes.bfloat16).astype(np.float64), axis, -1)
    blocks = v.reshape(v.shape[:-1] + (-1, 32))
    amax = np.abs(blocks).max(-1, keepdims=True)
    byte = np.maximum(np.where(amax > 0, np.frexp(amax)[1] - 1 + 127, 0) - down, 1)
    scale = np.exp2(byte - 127.0)
    codes = (blocks / scale).astype(np.float32).astype(dtype).astype(np.float64)
    return np.moveaxis((codes * scale).reshape(v.shape), -1, axis)


WIDE = False


def mx_kscale(k):
    if not WIDE:
        return np.ones(k)
    levels = np.array([10, -10, 5, -5, 0])
    if k % 512:
        return np.exp2(np.random.permutation(np.resize(levels, k // 32))).repeat(32)
    a = np.empty((k // 512, 16))
    for p in range(k // 512):
        a[p, :8] = np.random.permutation(np.resize(levels, 8))
        for g in range(8):
            far = levels[np.abs(levels - a[p, g]) >= 10]
            a[p, g + 8] = far[np.random.randint(len(far))]
    return np.exp2(a.ravel()).repeat(32)


def f64(x):
    return np.asarray(x).astype(np.float64)


def striped(idx):
    return np.tile(np.asarray(idx).reshape(-1, 16).T, (8, 1)).astype(np.uint16)


def unstriped(offs):
    return offs[:16].T.reshape(-1).astype(np.int64)


E2M1 = np.array([0.0, 0.5, 1.0, 1.5, 2.0, 3.0, 4.0, 6.0, -0.0, -0.5, -1.0, -1.5, -2.0, -3.0, -4.0, -6.0])


def pack_weight(w, fmt):
    k, n = w.shape
    w = f64(np.asarray(w, np.float32).astype(ml_dtypes.bfloat16)).reshape(k // 32, 32, n)
    amax = np.abs(w).max(1)
    if fmt == "e4m3":
        byte = np.frexp(amax)[1] - 1 + 127 - 7
    else:
        mant, ex = np.frexp(amax / 6.0)
        byte = np.where(mant > 0.5, ex, ex - 1) + 127
    byte = np.clip(np.where(amax > 0, byte, 1), 1, 254)
    scaled = (w * np.exp2(127.0 - byte)[:, None, :]).reshape(k, n).astype(np.float32)
    by_word = np.ascontiguousarray(scaled.reshape(k // 512, 128, 4, n).transpose(0, 1, 3, 2))
    if fmt == "e4m3":
        words = by_word.astype(ml_dtypes.float8_e4m3fn).view(np.uint8)
    else:
        c = by_word.astype(ml_dtypes.float4_e2m1fn).view(np.uint8) & 0xF
        words = (c[..., 0::2] | (c[..., 1::2] << 4)).reshape(k // 512, 128, 2 * n)
    return np.ascontiguousarray(words), np.ascontiguousarray(byte.astype(np.uint8).reshape(k // 512, 16, n))


def unpack_weight(words, scales, fmt):
    g, _, n = scales.shape
    words = np.ascontiguousarray(words).reshape(g, 128, n, -1)
    if fmt == "e4m3":
        vals = words.view(ml_dtypes.float8_e4m3fn).astype(np.float64)
    else:
        nib = np.empty((g, 128, n, 4), np.uint8)
        nib[..., 0::2] = words & 0xF
        nib[..., 1::2] = words >> 4
        vals = E2M1[nib]
    vals = vals * np.repeat(np.exp2(scales.astype(np.float64) - 127.0), 8, axis=1)[..., None]
    return vals.transpose(0, 1, 3, 2).reshape(g * 512, n)


def sigmoid(v):
    return 1.0 / (1.0 + np.exp(-v))


def bf(x):
    return np.asarray(x, np.float32).astype(ml_dtypes.bfloat16)


def planes(Y):
    r, m = Y.shape
    b = f64(bf(Y)).reshape(r // 32, 32, m)
    amax = np.abs(b).max(1)
    byte = np.clip(np.where(amax > 0, np.frexp(amax)[1] - 1 + 127 - 7, 1), 1, 254)
    codes = (b * np.exp2(127.0 - byte)[:, None, :]).reshape(r, m).astype(np.float32).astype(ml_dtypes.float8_e4m3fn).view(np.uint8)
    words = codes.reshape(r // 512, 128, 4, m).transpose(0, 1, 3, 2)
    return np.ascontiguousarray(words), np.ascontiguousarray(byte.astype(np.uint8).reshape(r // 512, 16, m))


D, E, T, I, Q = 512, 512, 2048, 512, 256


def setup_inputs():
    n = np.random.standard_normal
    idx = np.random.permutation(T)[:I]
    fd = mx_kscale(D)
    fe = mx_kscale(E)
    fi = mx_kscale(I)
    ti = np.ones(T)
    ti[idx] = fi
    keysp = pack_weight(n((D, T)) / fd[:, None], "e2m1")
    valsp = pack_weight(n((E, T)) / fe[:, None], "e2m1")
    return {
        "query": (n((D, Q)) * 0.8 / np.sqrt(D) * fd[:, None]).astype(np.float32),
        "query2": (n((D, Q)) * 0.8 / np.sqrt(D) * fd[:, None]).astype(np.float32),
        "keys_words": keysp[0],
        "keys_scales": keysp[1],
        "ba": (np.random.uniform(-1.0, 0.5, (Q, 1))).astype(np.float32),
        "bb": (np.random.uniform(-1.0, 0.5, (Q, 1))).astype(np.float32),
        "gout": (n((E, Q)) * 1 / np.sqrt(E) * fe[:, None]).astype(np.float32),
        "vals_words": valsp[0],
        "vals_scales": valsp[1],
        "fs": (np.random.uniform(128.0, 512.0, (1, I)) * fi).astype(np.float32),
        "keyrows": (n((D, T)) / ti).astype(np.float32),
        "res": (n((D, Q)) * 4.0).astype(np.float32),
        "offs": striped(idx),
    }


def reference(query, query2, keys_words, keys_scales, ba, bb, gout, vals_words, vals_scales, fs, keyrows, res, offs):
    idx = unstriped(offs)
    keysu = unpack_weight(keys_words, keys_scales, "e2m1")
    valsu = unpack_weight(vals_words, vals_scales, "e2m1")
    queryq = mxq(f64(query), 0, "e4m3")
    keysidxg = keysu[:, idx]
    a = queryq.T @ keysidxg
    query2q = mxq(f64(query2), 0, "e4m3")
    b = query2q.T @ keysidxg
    u1 = sigmoid(a + f64(ba))
    p = u1 * sigmoid(b + f64(bb))
    w = p / np.sum(p, axis=1, keepdims=True)
    goutq = mxq(f64(gout), 0, "e4m3")
    valsidxg = valsu[:, idx]
    dp = goutq.T @ valsidxg
    ds = w * (dp - np.sum(w * dp, axis=1, keepdims=True)) * (1.0 - u1) * f64(fs)
    dt = ds.T
    kt = f64(keyrows)[:, idx].T
    ktq = mxq(kt, 0, "e4m3")
    dtq = mxq(dt, 0, "e4m3")
    gq = ktq.T @ dtq
    y = gq + f64(res)
    words, scales = planes(y)
    return y, words, scales

@@ -1,0 +1,229 @@
+from contextlib import ExitStack
+
+import concourse.mybir as mybir
+
+D, E, T, I, Q = 512, 512, 2048, 512, 256
+FLOPS = 2 * Q * I * (2 * D + E) + 2 * D * Q * I
+
+F32 = mybir.dt.float32
+BF16 = mybir.dt.bfloat16
+I32 = mybir.dt.int32
+U32 = mybir.dt.uint32
+U16 = mybir.dt.uint16
+U8 = mybir.dt.uint8
+FP8X4 = mybir.dt.float8_e4m3fn_x4
+FP4X4 = mybir.dt.float4_e2m1fn_x4
+ALU = mybir.AluOpType
+ACT = mybir.ActivationFunctionType
+
+P = 128
+PACK = 4
+QT = Q // P
+
+
+def tile_attend_gbothquestions_pl_kernel(tc, query, query2, keys_words, keys_scales, ba, bb, gout,
+                                          vals_words, vals_scales, fs, keyrows, res, offs,
+                                          out_0, out_1, out_2):
+    nc = tc.nc
+    with ExitStack() as ctx:
+        sb = ctx.enter_context(tc.tile_pool(name="sb", bufs=1))
+        stage = ctx.enter_context(tc.tile_pool(name="stage", bufs=1))
+        ps = ctx.enter_context(tc.psum_pool(name="ps", bufs=1))
+
+        def tile(shape, dtype, name, tag=None):
+            return sb.tile(shape, dtype, name=name, tag=tag or name, align_bytes=64)
+
+        def bank(shape, b, name):
+            return ps.tile(shape, F32, name=name, tag=f"bank{b}")
+
+        offsets = sb.tile([P, I // 16], U16, name="offsets")
+        nc.sync.dma_start(offsets[:], offs)
+
+        key_scale_pool = tile([P, T], U8, "key_scale_pool")
+        nc.gpsimd.memset(key_scale_pool[:].bitcast(I32), 0)
+
+        rows_bytes = PACK * Q * 4
+        plane_bytes = T * 4
+        small_bytes = 64
+        early_bytes = 3 * rows_bytes + plane_bytes + T + 2 * small_bytes
+        late_bytes = (PACK - 1) * plane_bytes + rows_bytes + small_bytes
+        zeros = stage.tile([P, early_bytes // 4], F32, name="zeros", offset=0)
+        warm = stage.tile([P, late_bytes // 4], F32, name="warm", offset=early_bytes)
+        ident = tile([P, P], F32, "ident")
+        nc.gpsimd.memset(zeros[:, 0:P], 0.0)
+        nc.gpsimd.affine_select(out=ident[:], in_=zeros[:, 0:P], pattern=[[-1, P]], compare_op=ALU.not_equal,
+                                fill=1.0, base=0, channel_multiplier=1)
+        nc.scalar.activation(warm[:, 0:1], ident[:, 0:1], ACT.Sigmoid)
+        used = [0]
+        where = {}
+
+        def staged(shape, dtype, name, nbytes):
+            placed = stage.tile(shape, dtype, name=name, offset=used[0], align_bytes=64)
+            where[name] = used[0]
+            used[0] += nbytes
+            return placed
+
+        def load_scales(pool, src):
+            for quad in range(4):
+                nc.sync.dma_start(pool[32 * quad:32 * quad + 4, :].bitcast(I32),
+                                  src[0, 4 * quad:4 * quad + 4, :].bitcast(I32))
+
+        def load_rows(src, raw):
+            nc.sync.dma_start(raw[:], src.rearrange("(p j) q -> p j q", j=PACK))
+            return raw
+
+        def load_bias(src, name):
+            cols = staged([P, QT], F32, name, small_bytes)
+            with nc.allow_non_contiguous_dma(reason="one bias a partition"):
+                nc.sync.dma_start(cols[:], src.rearrange("(h p) o -> p (h o)", p=P))
+            return cols
+
+        keyrow_planes = keyrows.rearrange("(p j) t -> j p t", j=PACK)
+
+        def load_plane(j):
+            plane = staged([P, T], F32, f"plane_pool{j}", plane_bytes)
+            nc.sync.dma_start(plane[:], keyrow_planes[j])
+            return plane
+
+        key_word_pool = tile([P, T], U16, "key_word_pool")
+        nc.sync.dma_start(key_word_pool[:].bitcast(I32), keys_words[0].bitcast(I32))
+        query_raw = load_rows(query, tile([P, PACK, Q], F32, "query_raw"))
+        load_scales(key_scale_pool, keys_scales)
+        ba_cols = load_bias(ba, "ba_cols")
+        query2_raw = load_rows(query2, staged([P, PACK, Q], F32, "query2_raw", rows_bytes))
+        val_word_pool = staged([P, T], U16, "val_word_pool", rows_bytes)
+        nc.sync.dma_start(val_word_pool[:].bitcast(I32), vals_words[0].bitcast(I32))
+        bb_cols = load_bias(bb, "bb_cols")
+        gout_raw = load_rows(gout, staged([P, PACK, Q], F32, "gout_raw", rows_bytes))
+        plane_pool = [load_plane(0)]
+        val_scale_pool = staged([P, T], U8, "val_scale_pool", T)
+        nc.gpsimd.memset(val_scale_pool[:].bitcast(I32), 0)
+        load_scales(val_scale_pool, vals_scales)
+        fs_cols = staged([P, PACK], F32, "fs_cols", small_bytes)
+        nc.sync.dma_start(fs_cols[:], fs.rearrange("o (s r) -> (o s) r", r=PACK))
+        plane_pool.extend(load_plane(j) for j in range(1, PACK))
+        res_raw = load_rows(res, staged([P, PACK, Q], F32, "res_raw", rows_bytes))
+        neg_ba = tile([P, QT], F32, "neg_ba")
+        nc.gpsimd.tensor_scalar(neg_ba[:], ba_cols[:], -1.0, 0.0, ALU.mult, ALU.add)
+
+        def on_bytes_of(earlier, shape, dtype, name, skip=0):
+            return stage.tile(shape, dtype, name=name, offset=where[earlier] + skip, align_bytes=64)
+
+        def gather(pool, picked):
+            nc.vector.tensor_copy(picked[:], pool[:].indirect(offsets[:]))
+            return picked
+
+        def interleave(raw, grouped, engine_copy):
+            engine_copy(grouped.rearrange("p (c i j) -> p c j i", i=4, j=PACK),
+                        raw[:].rearrange("p j (c i) -> p c j i", i=4))
+            return grouped
+
+        def quantize(grouped, width, name):
+            codes = tile([P, width], U32, name + "_codes")
+            scales = tile([P, width], U8, name + "_scales")
+            nc.vector.quantize_mx(out=codes[:].bitcast(FP8X4), scales=scales[:], in_=grouped)
+            return codes, scales
+
+        def score(b, operand, h, words, scales, name):
+            acc = bank([P, I], b, name)
+            cols = slice(h * P, (h + 1) * P)
+            nc.tensor.matmul_mx(out=acc[:], lhsT=operand[0][:, cols].bitcast(FP8X4), lhsT_scale=operand[1][:, cols],
+                                rhs=words[:].bitcast(FP4X4), rhs_scale=scales[:], start=True, stop=True)
+            return acc[:].rearrange("q (s r) -> q r s", r=PACK)
+
+        key_words = gather(key_word_pool, tile([P, I], U16, "key_words"))
+        key_scales = gather(key_scale_pool, tile([P, I], U8, "key_scales"))
+        query_g = interleave(query_raw, tile([P, Q * PACK], BF16, "query_g")[:], nc.scalar.copy)
+        query_q = quantize(query_g, Q, "query")
+        query2_g = interleave(query2_raw, staged([P, 2 * Q * PACK], BF16, "query2_g", rows_bytes)[:, 0:Q * PACK],
+                              nc.vector.tensor_copy)
+        query2_q = quantize(query2_g, Q, "query2")
+        val_words = gather(val_word_pool, on_bytes_of("query2_g", [P, I], U16, "val_words", 2 * Q * PACK))
+
+        def dealt(name):
+            return [tile([P, PACK, P], F32, f"{name}{h}") for h in range(QT)]
+
+        a = [score(2 * h, query_q, h, key_words, key_scales, f"a{h}") for h in range(QT)]
+        b = [score(2 * h + 1, query2_q, h, key_words, key_scales, f"b{h}") for h in range(QT)]
+        u1, u2, v, p, pd, c, ds = (dealt(n) for n in ("u1_", "u2_", "v", "p", "pd", "c", "ds"))
+        for h in range(QT):
+            nc.scalar.activation(u1[h][:], a[h], ACT.Sigmoid, bias=ba_cols[:, h:h + 1])
+        for h in range(QT):
+            nc.scalar.activation(u2[h][:], b[h], ACT.Sigmoid, bias=bb_cols[:, h:h + 1])
+        gout_g = interleave(gout_raw, on_bytes_of("query2_g", [P, Q * PACK], BF16, "gout_g")[:], nc.scalar.copy)
+        for h in range(QT):
+            nc.scalar.activation(v[h][:], a[h], ACT.Sigmoid, bias=neg_ba[:, h:h + 1], scale=-1.0)
+
+        sum_p = tile([P, QT], F32, "sum_p")
+        sum_pd = tile([P, QT], F32, "sum_pd")
+        inv = tile([P, QT], F32, "inv")
+        mean = tile([P, QT], F32, "mean")
+        for h in range(QT):
+            nc.vector.scalar_tensor_tensor(p[h][:], u1[h][:], 1.0, u2[h][:], ALU.mult, ALU.mult,
+                                           accum_out=sum_p[:, h:h + 1])
+        val_scales = gather(val_scale_pool, tile([P, I], U8, "val_scales", "u2_0"))
+        gout_q = quantize(gout_g, Q, "gout")
+        nc.vector.reciprocal(inv[:], sum_p[:])
+        dp = [score(4 + h, gout_q, h, val_words, val_scales, f"dp{h}") for h in range(QT)]
+        for h in range(QT):
+            nc.vector.scalar_tensor_tensor(c[h][:], p[h][:], inv[:, h:h + 1], v[h][:], ALU.mult, ALU.mult)
+        for h in range(QT):
+            nc.vector.scalar_tensor_tensor(pd[h][:], p[h][:], 1.0, dp[h], ALU.mult, ALU.mult,
+                                           accum_out=sum_pd[:, h:h + 1])
+        nc.vector.tensor_tensor(mean[:], sum_pd[:], inv[:], ALU.mult)
+
+        plane0_bf = on_bytes_of("gout_raw", [P, T], BF16, "plane0_bf")
+        nc.scalar.activation(plane0_bf[:], plane_pool[0][:], ACT.Copy)
+        picked = [None] * PACK
+        picked[0] = tile([P, I], BF16, "plane0")
+        nc.scalar.activation(picked[0][:], plane0_bf[:].indirect(offsets[:]), ACT.Copy)
+
+        dt_turned = [bank([P, 2, Q], 6 + x, f"dt_turned{x}") for x in range(2)]
+        for h in range(QT):
+            nc.vector.scalar_tensor_tensor(ds[h][:], dp[h], mean[:, h:h + 1], c[h][:], ALU.subtract, ALU.mult)
+            for r in range(PACK):
+                nc.tensor.transpose(dt_turned[r // 2][:, r % 2, h * P:(h + 1) * P], ds[h][:, r, :], ident[:])
+        dt_rows = tile([P, PACK, Q], BF16, "dt_rows")
+        for r in range(PACK):
+            nc.scalar.activation(dt_rows[:, r, :], dt_turned[r // 2][:, r % 2, :], ACT.Copy, scale=fs_cols[:, r:r + 1])
+        dt_g = interleave(dt_rows, tile([P, Q * PACK], BF16, "dt_g")[:], nc.scalar.copy)
+
+        kt_g = [tile([P, P * PACK], BF16, f"kt_g{j}") for j in range(PACK)]
+        kt_q = [None] * PACK
+
+        def plane_turn(j):
+            words = picked[j][:].bitcast(F32)
+            xt = bank([P, 2, P], j, f"kt_turned{j}")
+            for u in range(2):
+                nc.tensor.transpose(xt[:, u, :], words[:, u:I // 2:2], ident[:])
+            nc.scalar.copy(kt_g[j][:].bitcast(F32).rearrange("s (c u) -> s c u", u=2),
+                           xt[:].rearrange("s u c -> s c u"))
+
+        def plane_quantize(j):
+            kt_q[j] = quantize(kt_g[j][:], P, f"kt{j}")
+
+        plane_turn(0)
+        for j in range(1, PACK):
+            picked[j] = gather(plane_pool[j], tile([P, I], BF16, f"plane{j}", f"c{(j - 1) % QT}"))
+            plane_turn(j)
+            plane_quantize(j - 1)
+        dt_q = quantize(dt_g, Q, "dt")
+
+        y = tile([P, PACK, Q], F32, "y")
+        y_out = out_0.rearrange("(p j) q -> p j q", j=PACK)
+        for j in range(PACK):
+            if j == PACK - 1:
+                plane_quantize(j)
+            gq = bank([P, Q], 4 + j, f"gq{j}")
+            nc.tensor.matmul_mx(out=gq[:], lhsT=kt_q[j][0][:].bitcast(FP8X4), lhsT_scale=kt_q[j][1][:],
+                                rhs=dt_q[0][:].bitcast(FP8X4), rhs_scale=dt_q[1][:], start=True, stop=True)
+            nc.vector.tensor_tensor(y[:, j, :], gq[:], res_raw[:, j, :], ALU.add)
+            nc.sync.dma_start(y_out[:, j, :], y[:, j, :])
+
+        y_g = interleave(y, tile([P, Q * PACK], BF16, "y_g")[:], nc.vector.tensor_copy)
+        y_codes, y_scales = quantize(y_g, Q, "y")
+        nc.sync.dma_start(out_1[0].rearrange("p c r -> p (c r)").bitcast(I32), y_codes[:].bitcast(I32))
+        for quad in range(4):
+            queue = nc.scalar if quad % 2 == 0 else nc.sync
+            queue.dma_start(out_2[0, 4 * quad:4 * quad + 4, :].bitcast(I32),
+                            y_scales[32 * quad:32 * quad + 4, :].bitcast(I32))

@@ -45,8 +45,8 @@ def tile_attend_gbothquestions_pl_kernel(tc, query, query2, keys_words, keys_sca
         rows_bytes = PACK * Q * 4
         plane_bytes = T * 4
         small_bytes = 64
-        early_bytes = 3 * rows_bytes + plane_bytes + T + 2 * small_bytes
-        late_bytes = (PACK - 1) * plane_bytes + rows_bytes + small_bytes
+        early_bytes = 3 * rows_bytes + T + 2 * small_bytes
+        late_bytes = PACK * plane_bytes + rows_bytes + small_bytes
         zeros = stage.tile([P, early_bytes // 4], F32, name="zeros", offset=0)
         warm = stage.tile([P, late_bytes // 4], F32, name="warm", offset=early_bytes)
         ident = tile([P, P], F32, "ident")
@@ -74,8 +74,7 @@ def tile_attend_gbothquestions_pl_kernel(tc, query, query2, keys_words, keys_sca
 
         def load_bias(src, name):
             cols = staged([P, QT], F32, name, small_bytes)
-            with nc.allow_non_contiguous_dma(reason="one bias a partition"):
-                nc.sync.dma_start(cols[:], src.rearrange("(h p) o -> p (h o)", p=P))
+            nc.sync.dma_start(cols[:], src.rearrange("(p h) o -> p (h o)", h=QT))
             return cols
 
         keyrow_planes = keyrows.rearrange("(p j) t -> j p t", j=PACK)
@@ -89,22 +88,22 @@ def tile_attend_gbothquestions_pl_kernel(tc, query, query2, keys_words, keys_sca
         nc.sync.dma_start(key_word_pool[:].bitcast(I32), keys_words[0].bitcast(I32))
         query_raw = load_rows(query, tile([P, PACK, Q], F32, "query_raw"))
         load_scales(key_scale_pool, keys_scales)
-        ba_cols = load_bias(ba, "ba_cols")
         query2_raw = load_rows(query2, staged([P, PACK, Q], F32, "query2_raw", rows_bytes))
+        ba_cols = load_bias(ba, "ba_cols")
         val_word_pool = staged([P, T], U16, "val_word_pool", rows_bytes)
         nc.sync.dma_start(val_word_pool[:].bitcast(I32), vals_words[0].bitcast(I32))
         bb_cols = load_bias(bb, "bb_cols")
         gout_raw = load_rows(gout, staged([P, PACK, Q], F32, "gout_raw", rows_bytes))
-        plane_pool = [load_plane(0)]
         val_scale_pool = staged([P, T], U8, "val_scale_pool", T)
         nc.gpsimd.memset(val_scale_pool[:].bitcast(I32), 0)
         load_scales(val_scale_pool, vals_scales)
+        plane_pool = [load_plane(0)]
         fs_cols = staged([P, PACK], F32, "fs_cols", small_bytes)
         nc.sync.dma_start(fs_cols[:], fs.rearrange("o (s r) -> (o s) r", r=PACK))
         plane_pool.extend(load_plane(j) for j in range(1, PACK))
         res_raw = load_rows(res, staged([P, PACK, Q], F32, "res_raw", rows_bytes))
-        neg_ba = tile([P, QT], F32, "neg_ba")
-        nc.gpsimd.tensor_scalar(neg_ba[:], ba_cols[:], -1.0, 0.0, ALU.mult, ALU.add)
+        neg_ba = staged([P, T // 2], F32, "neg_ba", 2 * T)[:, 0:QT]
+        nc.gpsimd.tensor_scalar(neg_ba, ba_cols[:], -1.0, 0.0, ALU.mult, ALU.add)
 
         def on_bytes_of(earlier, shape, dtype, name, skip=0):
             return stage.tile(shape, dtype, name=name, offset=where[earlier] + skip, align_bytes=64)
@@ -118,8 +117,16 @@ def tile_attend_gbothquestions_pl_kernel(tc, query, query2, keys_words, keys_sca
                         raw[:].rearrange("p j (c i) -> p c j i", i=4))
             return grouped
 
-        def quantize(grouped, width, name):
-            codes = tile([P, width], U32, name + "_codes")
+        def interleave_dealt(raw, grouped, engine_copy):
+            engine_copy(grouped.rearrange("p (h c m j) -> p c j m h", h=QT, m=2, j=PACK),
+                           raw[:].rearrange("p j (c m h) -> p c j m h", m=2, h=QT))
+            return grouped
+
+        def quantize(grouped, width, name, skip=None):
+            if skip is None:
+                codes = tile([P, width], U32, name + "_codes")
+            else:
+                codes = on_bytes_of("plane_pool3", [P, width], U32, name + "_codes", skip)
             scales = tile([P, width], U8, name + "_scales")
             nc.vector.quantize_mx(out=codes[:].bitcast(FP8X4), scales=scales[:], in_=grouped)
             return codes, scales
@@ -133,92 +140,101 @@ def tile_attend_gbothquestions_pl_kernel(tc, query, query2, keys_words, keys_sca
 
         key_words = gather(key_word_pool, tile([P, I], U16, "key_words"))
         key_scales = gather(key_scale_pool, tile([P, I], U8, "key_scales"))
-        query_g = interleave(query_raw, tile([P, Q * PACK], BF16, "query_g")[:], nc.scalar.copy)
+        query_g = interleave_dealt(query_raw, tile([P, Q * PACK], BF16, "query_g")[:], nc.scalar.copy)
         query_q = quantize(query_g, Q, "query")
-        query2_g = interleave(query2_raw, staged([P, 2 * Q * PACK], BF16, "query2_g", rows_bytes)[:, 0:Q * PACK],
-                              nc.vector.tensor_copy)
+        query2_g = interleave_dealt(query2_raw, staged([P, 2 * Q * PACK], BF16, "query2_g", rows_bytes)[:, 0:Q * PACK],
+                                    nc.vector.tensor_copy)
         query2_q = quantize(query2_g, Q, "query2")
         val_words = gather(val_word_pool, on_bytes_of("query2_g", [P, I], U16, "val_words", 2 * Q * PACK))
+        gout_g = interleave_dealt(gout_raw, on_bytes_of("query2_g", [P, Q * PACK], BF16, "gout_g")[:],
+                                  nc.vector.tensor_copy)
+        val_scales = gather(val_scale_pool, on_bytes_of("query2_g", [P, I], U8, "val_scales", 2 * Q * PACK + 2 * I))
+        gout_q = quantize(gout_g, Q, "gout")
 
         def dealt(name):
             return [tile([P, PACK, P], F32, f"{name}{h}") for h in range(QT)]
 
         a = [score(2 * h, query_q, h, key_words, key_scales, f"a{h}") for h in range(QT)]
         b = [score(2 * h + 1, query2_q, h, key_words, key_scales, f"b{h}") for h in range(QT)]
-        u1, u2, v, p, pd, c, ds = (dealt(n) for n in ("u1_", "u2_", "v", "p", "pd", "c", "ds"))
+        u1, u2, v, p, pd, ds = (dealt(n) for n in ("u1_", "u2_", "v", "p", "pd", "ds"))
+        c = [tile([P, PACK, P], F32, "c0"), staged([P, 6, P], F32, "c1", 6 * I)[:, 0:PACK, :]]
         for h in range(QT):
             nc.scalar.activation(u1[h][:], a[h], ACT.Sigmoid, bias=ba_cols[:, h:h + 1])
         for h in range(QT):
             nc.scalar.activation(u2[h][:], b[h], ACT.Sigmoid, bias=bb_cols[:, h:h + 1])
-        gout_g = interleave(gout_raw, on_bytes_of("query2_g", [P, Q * PACK], BF16, "gout_g")[:], nc.scalar.copy)
         for h in range(QT):
             nc.scalar.activation(v[h][:], a[h], ACT.Sigmoid, bias=neg_ba[:, h:h + 1], scale=-1.0)
 
         sum_p = tile([P, QT], F32, "sum_p")
-        sum_pd = tile([P, QT], F32, "sum_pd")
         inv = tile([P, QT], F32, "inv")
         mean = tile([P, QT], F32, "mean")
         for h in range(QT):
             nc.vector.scalar_tensor_tensor(p[h][:], u1[h][:], 1.0, u2[h][:], ALU.mult, ALU.mult,
                                            accum_out=sum_p[:, h:h + 1])
-        val_scales = gather(val_scale_pool, tile([P, I], U8, "val_scales", "u2_0"))
-        gout_q = quantize(gout_g, Q, "gout")
         nc.vector.reciprocal(inv[:], sum_p[:])
         dp = [score(4 + h, gout_q, h, val_words, val_scales, f"dp{h}") for h in range(QT)]
         for h in range(QT):
-            nc.vector.scalar_tensor_tensor(c[h][:], p[h][:], inv[:, h:h + 1], v[h][:], ALU.mult, ALU.mult)
+            nc.vector.scalar_tensor_tensor(pd[h][:], p[h][:], inv[:, h:h + 1], dp[h], ALU.mult, ALU.mult,
+                                           accum_out=mean[:, h:h + 1])
         for h in range(QT):
-            nc.vector.scalar_tensor_tensor(pd[h][:], p[h][:], 1.0, dp[h], ALU.mult, ALU.mult,
-                                           accum_out=sum_pd[:, h:h + 1])
-        nc.vector.tensor_tensor(mean[:], sum_pd[:], inv[:], ALU.mult)
+            nc.vector.scalar_tensor_tensor(c[h][:, :, :], p[h][:], inv[:, h:h + 1], v[h][:], ALU.mult, ALU.mult)
 
-        plane0_bf = on_bytes_of("gout_raw", [P, T], BF16, "plane0_bf")
+        plane0_bf = on_bytes_of("neg_ba", [P, T], BF16, "plane0_bf")
         nc.scalar.activation(plane0_bf[:], plane_pool[0][:], ACT.Copy)
         picked = [None] * PACK
         picked[0] = tile([P, I], BF16, "plane0")
         nc.scalar.activation(picked[0][:], plane0_bf[:].indirect(offsets[:]), ACT.Copy)
 
-        dt_turned = [bank([P, 2, Q], 6 + x, f"dt_turned{x}") for x in range(2)]
+        dt_turned = [bank([P, PACK, P], 6 + h, f"dt_turned{h}") for h in range(QT)]
         for h in range(QT):
-            nc.vector.scalar_tensor_tensor(ds[h][:], dp[h], mean[:, h:h + 1], c[h][:], ALU.subtract, ALU.mult)
+            nc.vector.scalar_tensor_tensor(ds[h][:], dp[h], mean[:, h:h + 1], c[h][:, :, :], ALU.subtract, ALU.mult)
             for r in range(PACK):
-                nc.tensor.transpose(dt_turned[r // 2][:, r % 2, h * P:(h + 1) * P], ds[h][:, r, :], ident[:])
-        dt_rows = tile([P, PACK, Q], BF16, "dt_rows")
-        for r in range(PACK):
-            nc.scalar.activation(dt_rows[:, r, :], dt_turned[r // 2][:, r % 2, :], ACT.Copy, scale=fs_cols[:, r:r + 1])
-        dt_g = interleave(dt_rows, tile([P, Q * PACK], BF16, "dt_g")[:], nc.scalar.copy)
+                nc.tensor.transpose(dt_turned[h][:, r, :], ds[h][:, r, :], ident[:])
 
-        kt_g = [tile([P, P * PACK], BF16, f"kt_g{j}") for j in range(PACK)]
-        kt_q = [None] * PACK
+        groups = [(0, 1), (2,), (3,)]
+        kt_g = {}
+        for group in groups:
+            grouped = tile([P, len(group), P * PACK], BF16, f"kt_g{group[0]}")
+            for x, j in enumerate(group):
+                kt_g[j] = grouped[:, x, :]
+            kt_g[group] = grouped[:].rearrange("s x c -> s (x c)")
 
         def plane_turn(j):
             words = picked[j][:].bitcast(F32)
             xt = bank([P, 2, P], j, f"kt_turned{j}")
             for u in range(2):
                 nc.tensor.transpose(xt[:, u, :], words[:, u:I // 2:2], ident[:])
-            nc.scalar.copy(kt_g[j][:].bitcast(F32).rearrange("s (c u) -> s c u", u=2),
+            nc.scalar.copy(kt_g[j].bitcast(F32).rearrange("s (c u) -> s c u", u=2),
                            xt[:].rearrange("s u c -> s c u"))
 
-        def plane_quantize(j):
-            kt_q[j] = quantize(kt_g[j][:], P, f"kt{j}")
-
+        dt_g = on_bytes_of("plane_pool3", [P, Q * PACK], BF16, "dt_g", 4 * Q * PACK)[:]
         plane_turn(0)
         for j in range(1, PACK):
-            picked[j] = gather(plane_pool[j], tile([P, I], BF16, f"plane{j}", f"c{(j - 1) % QT}"))
+            picked[j] = gather(plane_pool[j], on_bytes_of("c1", [P, I], BF16, f"plane{j}", 2 * I * (j - 1)))
             plane_turn(j)
-            plane_quantize(j - 1)
-        dt_q = quantize(dt_g, Q, "dt")
+        for h in range(QT):
+            nc.vector.tensor_tensor(dt_g[:, h * I:(h + 1) * I].rearrange("s (m r) -> s m r", r=PACK),
+                                    dt_turned[h][:].rearrange("s r m -> s m r"),
+                                    fs_cols[:].unsqueeze(1).to_broadcast([P, P, PACK]), ALU.mult)
 
         y = tile([P, PACK, Q], F32, "y")
         y_out = out_0.rearrange("(p j) q -> p j q", j=PACK)
-        for j in range(PACK):
-            if j == PACK - 1:
-                plane_quantize(j)
-            gq = bank([P, Q], 4 + j, f"gq{j}")
-            nc.tensor.matmul_mx(out=gq[:], lhsT=kt_q[j][0][:].bitcast(FP8X4), lhsT_scale=kt_q[j][1][:],
-                                rhs=dt_q[0][:].bitcast(FP8X4), rhs_scale=dt_q[1][:], start=True, stop=True)
-            nc.vector.tensor_tensor(y[:, j, :], gq[:], res_raw[:, j, :], ALU.add)
-            nc.sync.dma_start(y_out[:, j, :], y[:, j, :])
+        kt_q = {groups[0]: quantize(kt_g[groups[0]], len(groups[0]) * P, "kt0", 0)}
+        dt_q = quantize(dt_g, Q, "dt", 4 * Q * len(groups))
+        for g, group in enumerate(groups):
+            if g + 1 < len(groups):
+                kt_q[groups[g + 1]] = quantize(kt_g[groups[g + 1]], len(groups[g + 1]) * P, f"kt{g + 1}", 4 * Q * (g + 1))
+            codes, scales = kt_q[group]
+            gq = bank([P, len(group), Q], 4 + g, f"gq{g}")
+            for x in range(len(group)):
+                cols = slice(x * P, (x + 1) * P)
+                nc.tensor.matmul_mx(out=gq[:, x, :], lhsT=codes[:, cols].bitcast(FP8X4), lhsT_scale=scales[:, cols],
+                                    rhs=dt_q[0][:].bitcast(FP8X4), rhs_scale=dt_q[1][:], start=True, stop=True)
+            rows = slice(group[0], group[-1] + 1)
+            nc.vector.tensor_tensor(y[:, rows, :].rearrange("p x (m h) -> p x m h", h=QT),
+                                    gq[:].rearrange("p x (h m) -> p x m h", h=QT),
+                                    res_raw[:, rows, :].rearrange("p x (m h) -> p x m h", h=QT), ALU.add)
+            nc.sync.dma_start(y_out[:, rows, :], y[:, rows, :])
 
         y_g = interleave(y, tile([P, Q * PACK], BF16, "y_g")[:], nc.vector.tensor_copy)
         y_codes, y_scales = quantize(y_g, Q, "y")

@@ -45,7 +45,7 @@ def tile_attend_gbothquestions_pl_kernel(tc, query, query2, keys_words, keys_sca
         rows_bytes = PACK * Q * 4
         plane_bytes = T * 4
         small_bytes = 64
-        early_bytes = 3 * rows_bytes + T + 2 * small_bytes
+        early_bytes = 3 * rows_bytes + T + 3 * small_bytes
         late_bytes = PACK * plane_bytes + rows_bytes + small_bytes
         zeros = stage.tile([P, early_bytes // 4], F32, name="zeros", offset=0)
         warm = stage.tile([P, late_bytes // 4], F32, name="warm", offset=early_bytes)
@@ -53,7 +53,6 @@ def tile_attend_gbothquestions_pl_kernel(tc, query, query2, keys_words, keys_sca
         nc.gpsimd.memset(zeros[:, 0:P], 0.0)
         nc.gpsimd.affine_select(out=ident[:], in_=zeros[:, 0:P], pattern=[[-1, P]], compare_op=ALU.not_equal,
                                 fill=1.0, base=0, channel_multiplier=1)
-        nc.scalar.activation(warm[:, 0:1], ident[:, 0:1], ACT.Sigmoid)
         used = [0]
         where = {}
 
@@ -89,21 +88,22 @@ def tile_attend_gbothquestions_pl_kernel(tc, query, query2, keys_words, keys_sca
         query_raw = load_rows(query, tile([P, PACK, Q], F32, "query_raw"))
         load_scales(key_scale_pool, keys_scales)
         query2_raw = load_rows(query2, staged([P, PACK, Q], F32, "query2_raw", rows_bytes))
-        ba_cols = load_bias(ba, "ba_cols")
         val_word_pool = staged([P, T], U16, "val_word_pool", rows_bytes)
         nc.sync.dma_start(val_word_pool[:].bitcast(I32), vals_words[0].bitcast(I32))
+        ba_cols = load_bias(ba, "ba_cols")
         bb_cols = load_bias(bb, "bb_cols")
         gout_raw = load_rows(gout, staged([P, PACK, Q], F32, "gout_raw", rows_bytes))
         val_scale_pool = staged([P, T], U8, "val_scale_pool", T)
         nc.gpsimd.memset(val_scale_pool[:].bitcast(I32), 0)
         load_scales(val_scale_pool, vals_scales)
+        warm_in = staged([P, 1], F32, "warm_in", small_bytes)
+        nc.gpsimd.memset(warm_in[:], 0.0)
+        nc.scalar.activation(warm[:, 0:1], warm_in[:], ACT.Sigmoid)
         plane_pool = [load_plane(0)]
         fs_cols = staged([P, PACK], F32, "fs_cols", small_bytes)
         nc.sync.dma_start(fs_cols[:], fs.rearrange("o (s r) -> (o s) r", r=PACK))
         plane_pool.extend(load_plane(j) for j in range(1, PACK))
         res_raw = load_rows(res, staged([P, PACK, Q], F32, "res_raw", rows_bytes))
-        neg_ba = staged([P, T // 2], F32, "neg_ba", 2 * T)[:, 0:QT]
-        nc.gpsimd.tensor_scalar(neg_ba, ba_cols[:], -1.0, 0.0, ALU.mult, ALU.add)
 
         def on_bytes_of(earlier, shape, dtype, name, skip=0):
             return stage.tile(shape, dtype, name=name, offset=where[earlier] + skip, align_bytes=64)
@@ -156,14 +156,15 @@ def tile_attend_gbothquestions_pl_kernel(tc, query, query2, keys_words, keys_sca
 
         a = [score(2 * h, query_q, h, key_words, key_scales, f"a{h}") for h in range(QT)]
         b = [score(2 * h + 1, query2_q, h, key_words, key_scales, f"b{h}") for h in range(QT)]
-        u1, u2, v, p, pd, ds = (dealt(n) for n in ("u1_", "u2_", "v", "p", "pd", "ds"))
-        c = [tile([P, PACK, P], F32, "c0"), staged([P, 6, P], F32, "c1", 6 * I)[:, 0:PACK, :]]
+        u1, u2, v = (dealt(n) for n in ("u1_", "u2_", "v"))
+        ds = [on_bytes_of(f"plane_pool{h + 1}", [P, PACK, P], F32, f"ds{h}") for h in range(QT)]
+        p = [on_bytes_of(earlier, [P, PACK, P], F32, f"p{h}") for h, earlier in enumerate(("val_scale_pool", "query2_g"))]
+        pd = [staged([P, PACK, P], F32, f"pd{h}", 4 * I) for h in range(QT)]
+        c = [staged([P, PACK, P], F32, f"c{h}", 4 * I) for h in range(QT)]
         for h in range(QT):
             nc.scalar.activation(u1[h][:], a[h], ACT.Sigmoid, bias=ba_cols[:, h:h + 1])
         for h in range(QT):
             nc.scalar.activation(u2[h][:], b[h], ACT.Sigmoid, bias=bb_cols[:, h:h + 1])
-        for h in range(QT):
-            nc.scalar.activation(v[h][:], a[h], ACT.Sigmoid, bias=neg_ba[:, h:h + 1], scale=-1.0)
 
         sum_p = tile([P, QT], F32, "sum_p")
         inv = tile([P, QT], F32, "inv")
@@ -172,26 +173,23 @@ def tile_attend_gbothquestions_pl_kernel(tc, query, query2, keys_words, keys_sca
             nc.vector.scalar_tensor_tensor(p[h][:], u1[h][:], 1.0, u2[h][:], ALU.mult, ALU.mult,
                                            accum_out=sum_p[:, h:h + 1])
         nc.vector.reciprocal(inv[:], sum_p[:])
+        neg_inv = staged([P, T // 2], F32, "neg_inv", 2 * T)[:, 0:QT]
+        nc.scalar.activation(neg_inv, inv[:], ACT.Copy, scale=-1.0)
         dp = [score(4 + h, gout_q, h, val_words, val_scales, f"dp{h}") for h in range(QT)]
         for h in range(QT):
             nc.vector.scalar_tensor_tensor(pd[h][:], p[h][:], inv[:, h:h + 1], dp[h], ALU.mult, ALU.mult,
                                            accum_out=mean[:, h:h + 1])
         for h in range(QT):
-            nc.vector.scalar_tensor_tensor(c[h][:, :, :], p[h][:], inv[:, h:h + 1], v[h][:], ALU.mult, ALU.mult)
+            nc.scalar.activation(v[h][:], u1[h][:], ACT.Identity, bias=inv[:, h:h + 1], scale=neg_inv[:, h:h + 1])
+            nc.gpsimd.tensor_tensor(c[h][:], v[h][:], p[h][:], ALU.mult)
 
-        plane0_bf = on_bytes_of("neg_ba", [P, T], BF16, "plane0_bf")
+        plane0_bf = on_bytes_of("neg_inv", [P, T], BF16, "plane0_bf")
         nc.scalar.activation(plane0_bf[:], plane_pool[0][:], ACT.Copy)
         picked = [None] * PACK
         picked[0] = tile([P, I], BF16, "plane0")
         nc.scalar.activation(picked[0][:], plane0_bf[:].indirect(offsets[:]), ACT.Copy)
 
-        dt_turned = [bank([P, PACK, P], 6 + h, f"dt_turned{h}") for h in range(QT)]
-        for h in range(QT):
-            nc.vector.scalar_tensor_tensor(ds[h][:], dp[h], mean[:, h:h + 1], c[h][:, :, :], ALU.subtract, ALU.mult)
-            for r in range(PACK):
-                nc.tensor.transpose(dt_turned[h][:, r, :], ds[h][:, r, :], ident[:])
-
-        groups = [(0, 1), (2,), (3,)]
+        groups = [(0, 1), (2, 3)]
         kt_g = {}
         for group in groups:
             grouped = tile([P, len(group), P * PACK], BF16, f"kt_g{group[0]}")
@@ -201,17 +199,24 @@ def tile_attend_gbothquestions_pl_kernel(tc, query, query2, keys_words, keys_sca
 
         def plane_turn(j):
             words = picked[j][:].bitcast(F32)
-            xt = bank([P, 2, P], j, f"kt_turned{j}")
+            xt = bank([P, 2, P], j if j else 5, f"kt_turned{j}")
             for u in range(2):
                 nc.tensor.transpose(xt[:, u, :], words[:, u:I // 2:2], ident[:])
             nc.scalar.copy(kt_g[j].bitcast(F32).rearrange("s (c u) -> s c u", u=2),
                            xt[:].rearrange("s u c -> s c u"))
 
         dt_g = on_bytes_of("plane_pool3", [P, Q * PACK], BF16, "dt_g", 4 * Q * PACK)[:]
-        plane_turn(0)
+        dt_turned = [bank([P, PACK, P], 6 + h, f"dt_turned{h}") for h in range(QT)]
         for j in range(1, PACK):
-            picked[j] = gather(plane_pool[j], on_bytes_of("c1", [P, I], BF16, f"plane{j}", 2 * I * (j - 1)))
+            picked[j] = gather(plane_pool[j], on_bytes_of(("pd1", "c0", "c1")[j - 1], [P, I], BF16, f"plane{j}"))
+            if j == PACK - 1:
+                plane_turn(0)
             plane_turn(j)
+            h = j - 1
+            if h < QT:
+                nc.vector.scalar_tensor_tensor(ds[h][:], dp[h], mean[:, h:h + 1], c[h][:], ALU.subtract, ALU.mult)
+                for r in range(PACK):
+                    nc.tensor.transpose(dt_turned[h][:, r, :], ds[h][:, r, :], ident[:])
         for h in range(QT):
             nc.vector.tensor_tensor(dt_g[:, h * I:(h + 1) * I].rearrange("s (m r) -> s m r", r=PACK),
                                     dt_turned[h][:].rearrange("s r m -> s m r"),

from contextlib import ExitStack

import concourse.mybir as mybir

D, E, T, I, Q = 512, 512, 2048, 512, 256
FLOPS = 2 * Q * I * (2 * D + E) + 2 * D * Q * I

F32 = mybir.dt.float32
BF16 = mybir.dt.bfloat16
I32 = mybir.dt.int32
U32 = mybir.dt.uint32
U16 = mybir.dt.uint16
U8 = mybir.dt.uint8
FP8X4 = mybir.dt.float8_e4m3fn_x4
FP4X4 = mybir.dt.float4_e2m1fn_x4
ALU = mybir.AluOpType
ACT = mybir.ActivationFunctionType

P = 128
PACK = 4
QT = Q // P


def tile_attend_gbothquestions_pl_kernel(tc, query, query2, keys_words, keys_scales, ba, bb, gout,
                                          vals_words, vals_scales, fs, keyrows, res, offs,
                                          out_0, out_1, out_2):
    nc = tc.nc
    with ExitStack() as ctx:
        sb = ctx.enter_context(tc.tile_pool(name="sb", bufs=1))
        stage = ctx.enter_context(tc.tile_pool(name="stage", bufs=1))
        ps = ctx.enter_context(tc.psum_pool(name="ps", bufs=1))

        def tile(shape, dtype, name, tag=None):
            return sb.tile(shape, dtype, name=name, tag=tag or name, align_bytes=64)

        def bank(shape, b, name):
            return ps.tile(shape, F32, name=name, tag=f"bank{b}")

        offsets = sb.tile([P, I // 16], U16, name="offsets")
        nc.sync.dma_start(offsets[:], offs)

        key_scale_pool = tile([P, T], U8, "key_scale_pool")
        nc.gpsimd.memset(key_scale_pool[:].bitcast(I32), 0)

        rows_bytes = PACK * Q * 4
        plane_bytes = T * 4
        small_bytes = 64
        early_bytes = 3 * rows_bytes + T + 3 * small_bytes
        late_bytes = PACK * plane_bytes + rows_bytes + small_bytes
        zeros = stage.tile([P, early_bytes // 4], F32, name="zeros", offset=0)
        warm = stage.tile([P, late_bytes // 4], F32, name="warm", offset=early_bytes)
        ident = tile([P, P], F32, "ident")
        nc.gpsimd.memset(zeros[:, 0:P], 0.0)
        nc.gpsimd.affine_select(out=ident[:], in_=zeros[:, 0:P], pattern=[[-1, P]], compare_op=ALU.not_equal,
                                fill=1.0, base=0, channel_multiplier=1)
        used = [0]
        where = {}

        def staged(shape, dtype, name, nbytes):
            placed = stage.tile(shape, dtype, name=name, offset=used[0], align_bytes=64)
            where[name] = used[0]
            used[0] += nbytes
            return placed

        def load_scales(pool, src):
            for quad in range(4):
                nc.sync.dma_start(pool[32 * quad:32 * quad + 4, :].bitcast(I32),
                                  src[0, 4 * quad:4 * quad + 4, :].bitcast(I32))

        def load_rows(src, raw):
            nc.sync.dma_start(raw[:], src.rearrange("(p j) q -> p j q", j=PACK))
            return raw

        def load_bias(src, name):
            cols = staged([P, QT], F32, name, small_bytes)
            nc.sync.dma_start(cols[:], src.rearrange("(p h) o -> p (h o)", h=QT))
            return cols

        keyrow_planes = keyrows.rearrange("(p j) t -> j p t", j=PACK)

        def load_plane(j):
            plane = staged([P, T], F32, f"plane_pool{j}", plane_bytes)
            nc.sync.dma_start(plane[:], keyrow_planes[j])
            return plane

        key_word_pool = tile([P, T], U16, "key_word_pool")
        nc.sync.dma_start(key_word_pool[:].bitcast(I32), keys_words[0].bitcast(I32))
        query_raw = load_rows(query, tile([P, PACK, Q], F32, "query_raw"))
        load_scales(key_scale_pool, keys_scales)
        query2_raw = load_rows(query2, staged([P, PACK, Q], F32, "query2_raw", rows_bytes))
        val_word_pool = staged([P, T], U16, "val_word_pool", rows_bytes)
        nc.sync.dma_start(val_word_pool[:].bitcast(I32), vals_words[0].bitcast(I32))
        ba_cols = load_bias(ba, "ba_cols")
        bb_cols = load_bias(bb, "bb_cols")
        gout_raw = load_rows(gout, staged([P, PACK, Q], F32, "gout_raw", rows_bytes))
        val_scale_pool = staged([P, T], U8, "val_scale_pool", T)
        nc.gpsimd.memset(val_scale_pool[:].bitcast(I32), 0)
        load_scales(val_scale_pool, vals_scales)
        warm_in = staged([P, 1], F32, "warm_in", small_bytes)
        nc.gpsimd.memset(warm_in[:], 0.0)
        nc.scalar.activation(warm[:, 0:1], warm_in[:], ACT.Sigmoid)
        plane_pool = [load_plane(0)]
        fs_cols = staged([P, PACK], F32, "fs_cols", small_bytes)
        nc.sync.dma_start(fs_cols[:], fs.rearrange("o (s r) -> (o s) r", r=PACK))
        plane_pool.extend(load_plane(j) for j in range(1, PACK))
        res_raw = load_rows(res, staged([P, PACK, Q], F32, "res_raw", rows_bytes))

        def on_bytes_of(earlier, shape, dtype, name, skip=0):
            return stage.tile(shape, dtype, name=name, offset=where[earlier] + skip, align_bytes=64)

        def gather(pool, picked):
            nc.vector.tensor_copy(picked[:], pool[:].indirect(offsets[:]))
            return picked

        def interleave(raw, grouped, engine_copy):
            engine_copy(grouped.rearrange("p (c i j) -> p c j i", i=4, j=PACK),
                        raw[:].rearrange("p j (c i) -> p c j i", i=4))
            return grouped

        def interleave_dealt(raw, grouped, engine_copy):
            engine_copy(grouped.rearrange("p (h c m j) -> p c j m h", h=QT, m=2, j=PACK),
                           raw[:].rearrange("p j (c m h) -> p c j m h", m=2, h=QT))
            return grouped

        def quantize(grouped, width, name, skip=None):
            if skip is None:
                codes = tile([P, width], U32, name + "_codes")
            else:
                codes = on_bytes_of("plane_pool3", [P, width], U32, name + "_codes", skip)
            scales = tile([P, width], U8, name + "_scales")
            nc.vector.quantize_mx(out=codes[:].bitcast(FP8X4), scales=scales[:], in_=grouped)
            return codes, scales

        def score(b, operand, h, words, scales, name):
            acc = bank([P, I], b, name)
            cols = slice(h * P, (h + 1) * P)
            nc.tensor.matmul_mx(out=acc[:], lhsT=operand[0][:, cols].bitcast(FP8X4), lhsT_scale=operand[1][:, cols],
                                rhs=words[:].bitcast(FP4X4), rhs_scale=scales[:], start=True, stop=True)
            return acc[:].rearrange("q (s r) -> q r s", r=PACK)

        key_words = gather(key_word_pool, tile([P, I], U16, "key_words"))
        key_scales = gather(key_scale_pool, tile([P, I], U8, "key_scales"))
        query_g = interleave_dealt(query_raw, tile([P, Q * PACK], BF16, "query_g")[:], nc.scalar.copy)
        query_q = quantize(query_g, Q, "query")
        query2_g = interleave_dealt(query2_raw, staged([P, 2 * Q * PACK], BF16, "query2_g", rows_bytes)[:, 0:Q * PACK],
                                    nc.vector.tensor_copy)
        query2_q = quantize(query2_g, Q, "query2")
        val_words = gather(val_word_pool, on_bytes_of("query2_g", [P, I], U16, "val_words", 2 * Q * PACK))
        gout_g = interleave_dealt(gout_raw, on_bytes_of("query2_g", [P, Q * PACK], BF16, "gout_g")[:],
                                  nc.vector.tensor_copy)
        val_scales = gather(val_scale_pool, on_bytes_of("query2_g", [P, I], U8, "val_scales", 2 * Q * PACK + 2 * I))
        gout_q = quantize(gout_g, Q, "gout")

        def dealt(name):
            return [tile([P, PACK, P], F32, f"{name}{h}") for h in range(QT)]

        a = [score(2 * h, query_q, h, key_words, key_scales, f"a{h}") for h in range(QT)]
        b = [score(2 * h + 1, query2_q, h, key_words, key_scales, f"b{h}") for h in range(QT)]
        u1, u2, v = (dealt(n) for n in ("u1_", "u2_", "v"))
        ds = [on_bytes_of(f"plane_pool{h + 1}", [P, PACK, P], F32, f"ds{h}") for h in range(QT)]
        p = [on_bytes_of(earlier, [P, PACK, P], F32, f"p{h}") for h, earlier in enumerate(("val_scale_pool", "query2_g"))]
        pd = [staged([P, PACK, P], F32, f"pd{h}", 4 * I) for h in range(QT)]
        c = [staged([P, PACK, P], F32, f"c{h}", 4 * I) for h in range(QT)]
        for h in range(QT):
            nc.scalar.activation(u1[h][:], a[h], ACT.Sigmoid, bias=ba_cols[:, h:h + 1])
        for h in range(QT):
            nc.scalar.activation(u2[h][:], b[h], ACT.Sigmoid, bias=bb_cols[:, h:h + 1])

        sum_p = tile([P, QT], F32, "sum_p")
        inv = tile([P, QT], F32, "inv")
        mean = tile([P, QT], F32, "mean")
        for h in range(QT):
            nc.vector.scalar_tensor_tensor(p[h][:], u1[h][:], 1.0, u2[h][:], ALU.mult, ALU.mult,
                                           accum_out=sum_p[:, h:h + 1])
        nc.vector.reciprocal(inv[:], sum_p[:])
        neg_inv = staged([P, T // 2], F32, "neg_inv", 2 * T)[:, 0:QT]
        nc.scalar.activation(neg_inv, inv[:], ACT.Copy, scale=-1.0)
        dp = [score(4 + h, gout_q, h, val_words, val_scales, f"dp{h}") for h in range(QT)]
        for h in range(QT):
            nc.vector.scalar_tensor_tensor(pd[h][:], p[h][:], inv[:, h:h + 1], dp[h], ALU.mult, ALU.mult,
                                           accum_out=mean[:, h:h + 1])
        for h in range(QT):
            nc.scalar.activation(v[h][:], u1[h][:], ACT.Identity, bias=inv[:, h:h + 1], scale=neg_inv[:, h:h + 1])
            nc.gpsimd.tensor_tensor(c[h][:], v[h][:], p[h][:], ALU.mult)

        plane0_bf = on_bytes_of("neg_inv", [P, T], BF16, "plane0_bf")
        nc.scalar.activation(plane0_bf[:], plane_pool[0][:], ACT.Copy)
        picked = [None] * PACK
        picked[0] = tile([P, I], BF16, "plane0")
        nc.scalar.activation(picked[0][:], plane0_bf[:].indirect(offsets[:]), ACT.Copy)

        groups = [(0, 1), (2, 3)]
        kt_g = {}
        for group in groups:
            grouped = tile([P, len(group), P * PACK], BF16, f"kt_g{group[0]}")
            for x, j in enumerate(group):
                kt_g[j] = grouped[:, x, :]
            kt_g[group] = grouped[:].rearrange("s x c -> s (x c)")

        def plane_turn(j):
            words = picked[j][:].bitcast(F32)
            xt = bank([P, 2, P], j if j else 5, f"kt_turned{j}")
            for u in range(2):
                nc.tensor.transpose(xt[:, u, :], words[:, u:I // 2:2], ident[:])
            nc.scalar.copy(kt_g[j].bitcast(F32).rearrange("s (c u) -> s c u", u=2),
                           xt[:].rearrange("s u c -> s c u"))

        dt_g = on_bytes_of("plane_pool3", [P, Q * PACK], BF16, "dt_g", 4 * Q * PACK)[:]
        dt_turned = [bank([P, PACK, P], 6 + h, f"dt_turned{h}") for h in range(QT)]
        for j in range(1, PACK):
            picked[j] = gather(plane_pool[j], on_bytes_of(("pd1", "c0", "c1")[j - 1], [P, I], BF16, f"plane{j}"))
            if j == PACK - 1:
                plane_turn(0)
            plane_turn(j)
            h = j - 1
            if h < QT:
                nc.vector.scalar_tensor_tensor(ds[h][:], dp[h], mean[:, h:h + 1], c[h][:], ALU.subtract, ALU.mult)
                for r in range(PACK):
                    nc.tensor.transpose(dt_turned[h][:, r, :], ds[h][:, r, :], ident[:])
        for h in range(QT):
            nc.vector.tensor_tensor(dt_g[:, h * I:(h + 1) * I].rearrange("s (m r) -> s m r", r=PACK),
                                    dt_turned[h][:].rearrange("s r m -> s m r"),
                                    fs_cols[:].unsqueeze(1).to_broadcast([P, P, PACK]), ALU.mult)

        y = tile([P, PACK, Q], F32, "y")
        y_out = out_0.rearrange("(p j) q -> p j q", j=PACK)
        kt_q = {groups[0]: quantize(kt_g[groups[0]], len(groups[0]) * P, "kt0", 0)}
        dt_q = quantize(dt_g, Q, "dt", 4 * Q * len(groups))
        for g, group in enumerate(groups):
            if g + 1 < len(groups):
                kt_q[groups[g + 1]] = quantize(kt_g[groups[g + 1]], len(groups[g + 1]) * P, f"kt{g + 1}", 4 * Q * (g + 1))
            codes, scales = kt_q[group]
            gq = bank([P, len(group), Q], 4 + g, f"gq{g}")
            for x in range(len(group)):
                cols = slice(x * P, (x + 1) * P)
                nc.tensor.matmul_mx(out=gq[:, x, :], lhsT=codes[:, cols].bitcast(FP8X4), lhsT_scale=scales[:, cols],
                                    rhs=dt_q[0][:].bitcast(FP8X4), rhs_scale=dt_q[1][:], start=True, stop=True)
            rows = slice(group[0], group[-1] + 1)
            nc.vector.tensor_tensor(y[:, rows, :].rearrange("p x (m h) -> p x m h", h=QT),
                                    gq[:].rearrange("p x (h m) -> p x m h", h=QT),
                                    res_raw[:, rows, :].rearrange("p x (m h) -> p x m h", h=QT), ALU.add)
            nc.sync.dma_start(y_out[:, rows, :], y[:, rows, :])

        y_g = interleave(y, tile([P, Q * PACK], BF16, "y_g")[:], nc.vector.tensor_copy)
        y_codes, y_scales = quantize(y_g, Q, "y")
        nc.sync.dma_start(out_1[0].rearrange("p c r -> p (c r)").bitcast(I32), y_codes[:].bitcast(I32))
        for quad in range(4):
            queue = nc.scalar if quad % 2 == 0 else nc.sync
            queue.dma_start(out_2[0, 4 * quad:4 * quad + 4, :].bitcast(I32),
                            y_scales[32 * quad:32 * quad + 4, :].bitcast(I32))
